import numpy as np
import ml_dtypes

BF16 = ml_dtypes.bfloat16


def bf(x):
    return np.asarray(x, np.float32).astype(BF16)


def f32(x):
    return np.asarray(x, np.float32)


def f64(x):
    return np.asarray(x).astype(np.float64)


def striped(idx):
    return np.tile(idx.reshape(-1, 16).T, (8, 1))


S, K, M, N, E, Q = 256, 128, 256, 128, 2, 64


def setup_inputs():
    return {"base": bf(np.random.standard_normal((M, S))), "x": bf(np.random.standard_normal((K, N))), "w": bf(np.random.standard_normal((E, K, M)) / np.sqrt(K)), "b": f32(0.5 * np.random.standard_normal((M, 1))), "offs": striped(np.random.permutation(S)[:N])}


def reference(base, x, w, b, offs):
    idx = offs[:16].T.reshape(-1)
    z = f64(base).copy()
    for e in range(E):
        z[:, idx[e * Q : (e + 1) * Q]] = f64(w)[e].T @ f64(x)[:, e * Q : (e + 1) * Q]
    return np.tanh(z + f64(b))

@@ -1,0 +1,59 @@
+import concourse.mybir as mybir
+from concourse.masks import make_identity
+
+BF16, F32, U16 = mybir.dt.bfloat16, mybir.dt.float32, mybir.dt.uint16
+TANH = mybir.ActivationFunctionType.Tanh
+
+P = 128
+S = 256
+M = 256
+N = 128
+E = 2
+Q = N // E
+BLOCKS = M // P
+QC = Q // 16
+
+FLOPS = 2 * P * M * N
+
+
+def tile_scatter_matmul_kernel(tc, base, x, w, b, offs, out):
+    nc = tc.nc
+    with (
+        tc.tile_pool(name="held", bufs=1) as held,
+        tc.psum_pool(name="banks", bufs=1) as banks,
+    ):
+        offsets = held.tile([P, N // 16], U16, name="offsets")
+        nc.sync.dma_start(offsets[:], offs)
+
+        base_sb = held.tile([P, BLOCKS, S], BF16, name="base_sb")
+        nc.sync.dma_start(base_sb[:], base.rearrange("(a p) s -> p a s", p=P))
+
+        w_sb = held.tile([P, E, M], BF16, name="w_sb")
+        nc.scalar.dma_start(w_sb[:], w.rearrange("e k m -> k e m"))
+        x_sb = held.tile([P, N], BF16, name="x_sb")
+        nc.scalar.dma_start(x_sb[:], x)
+
+        bias = held.tile([P, BLOCKS], F32, name="bias")
+        nc.scalar.dma_start(bias[:], b.rearrange("(a p) o -> p (a o)", p=P))
+
+        ident = held.tile([P, P], BF16, name="ident")
+        make_identity(nc, ident[:])
+
+        windows = [banks.tile([P, S], F32, name=f"window{a}") for a in range(BLOCKS)]
+        for a in range(BLOCKS):
+            nc.tensor.matmul(windows[a][:], ident[:], base_sb[:, a, :], start=True, stop=True)
+
+        for a in range(BLOCKS):
+            for e in range(E):
+                nc.tensor.matmul(
+                    windows[a][:].indirect(offsets[:, e * QC : (e + 1) * QC]),
+                    w_sb[:, e, a * P : (a + 1) * P],
+                    x_sb[:, e * Q : (e + 1) * Q],
+                    start=True,
+                    stop=True,
+                )
+
+        for a in range(BLOCKS):
+            result = held.tile([P, S], F32, name=f"result{a}")
+            nc.scalar.activation(result[:], windows[a][:], TANH, bias=bias[:, a : a + 1])
+            nc.sync.dma_start(out[a * P : (a + 1) * P, :], result[:])

@@ -36,6 +36,11 @@ def tile_scatter_matmul_kernel(tc, base, x, w, b, offs, out):
         bias = held.tile([P, BLOCKS], F32, name="bias")
         nc.scalar.dma_start(bias[:], b.rearrange("(a p) o -> p (a o)", p=P))
 
+        zeros = held.tile([P, 1], F32, name="zeros")
+        nc.vector.memset(zeros[:], 0.0)
+        warmed = held.tile([P, 1], F32, name="warmed")
+        nc.scalar.activation(warmed[:], zeros[:], TANH)
+
         ident = held.tile([P, P], BF16, name="ident")
         make_identity(nc, ident[:])
 

@@ -22,11 +22,11 @@ def tile_scatter_matmul_kernel(tc, base, x, w, b, offs, out):
         tc.tile_pool(name="held", bufs=1) as held,
         tc.psum_pool(name="banks", bufs=1) as banks,
     ):
-        offsets = held.tile([P, N // 16], U16, name="offsets")
-        nc.sync.dma_start(offsets[:], offs)
-
         base_sb = held.tile([P, BLOCKS, S], BF16, name="base_sb")
         nc.sync.dma_start(base_sb[:], base.rearrange("(a p) s -> p a s", p=P))
+
+        offsets = held.tile([P, N // 16], U16, name="offsets")
+        nc.sync.dma_start(offsets[:], offs)
 
         w_sb = held.tile([P, E, M], BF16, name="w_sb")
         nc.scalar.dma_start(w_sb[:], w.rearrange("e k m -> k e m"))
@@ -34,7 +34,7 @@ def tile_scatter_matmul_kernel(tc, base, x, w, b, offs, out):
         nc.scalar.dma_start(x_sb[:], x)
 
         bias = held.tile([P, BLOCKS], F32, name="bias")
-        nc.scalar.dma_start(bias[:], b.rearrange("(a p) o -> p (a o)", p=P))
+        nc.sync.dma_start(bias[:], b.rearrange("(a p) o -> p (a o)", p=P))
 
         zeros = held.tile([P, 1], F32, name="zeros")
         nc.vector.memset(zeros[:], 0.0)

@@ -13,6 +13,8 @@ Q = N // E
 BLOCKS = M // P
 QC = Q // 16
 
+WARM = 6
+
 FLOPS = 2 * P * M * N
 
 
@@ -35,6 +37,12 @@ def tile_scatter_matmul_kernel(tc, base, x, w, b, offs, out):
 
         bias = held.tile([P, BLOCKS], F32, name="bias")
         nc.sync.dma_start(bias[:], b.rearrange("(a p) o -> p (a o)", p=P))
+
+        idle_sb = held.tile([P, S], BF16, name="idle_sb")
+        nc.vector.memset(idle_sb[:], 0.0)
+        idle_ps = banks.tile([P, S], F32, name="idle_ps")
+        for i in range(WARM):
+            nc.tensor.matmul(idle_ps[:], idle_sb[:, 0:P], idle_sb[:], start=True, stop=True)
 
         zeros = held.tile([P, 1], F32, name="zeros")
         nc.vector.memset(zeros[:], 0.0)

@@ -24,16 +24,17 @@ def tile_scatter_matmul_kernel(tc, base, x, w, b, offs, out):
         tc.tile_pool(name="held", bufs=1) as held,
         tc.psum_pool(name="banks", bufs=1) as banks,
     ):
+
         base_sb = held.tile([P, BLOCKS, S], BF16, name="base_sb")
         nc.sync.dma_start(base_sb[:], base.rearrange("(a p) s -> p a s", p=P))
 
         offsets = held.tile([P, N // 16], U16, name="offsets")
         nc.sync.dma_start(offsets[:], offs)
 
-        w_sb = held.tile([P, E, M], BF16, name="w_sb")
-        nc.scalar.dma_start(w_sb[:], w.rearrange("e k m -> k e m"))
         x_sb = held.tile([P, N], BF16, name="x_sb")
-        nc.scalar.dma_start(x_sb[:], x)
+        nc.sync.dma_start(x_sb[:], x)
+        w_sb = held.tile([P, E, M], BF16, name="w_sb")
+        nc.sync.dma_start(w_sb[:], w.rearrange("e k m -> k e m"))
 
         bias = held.tile([P, BLOCKS], F32, name="bias")
         nc.sync.dma_start(bias[:], b.rearrange("(a p) o -> p (a o)", p=P))

@@ -70,4 +70,5 @@ def tile_scatter_matmul_kernel(tc, base, x, w, b, offs, out):
         for a in range(BLOCKS):
             result = held.tile([P, S], F32, name=f"result{a}")
             nc.scalar.activation(result[:], windows[a][:], TANH, bias=bias[:, a : a + 1])
-            nc.sync.dma_start(out[a * P : (a + 1) * P, :], result[:])
+            store_queue = nc.scalar if a == BLOCKS - 1 else nc.sync
+            store_queue.dma_start(out[a * P : (a + 1) * P, :], result[:])

@@ -33,11 +33,15 @@ def tile_scatter_matmul_kernel(tc, base, x, w, b, offs, out):
 
         x_sb = held.tile([P, N], BF16, name="x_sb")
         nc.sync.dma_start(x_sb[:], x)
-        w_sb = held.tile([P, E, M], BF16, name="w_sb")
-        nc.sync.dma_start(w_sb[:], w.rearrange("e k m -> k e m"))
 
+        w_sb = [held.tile([P, E, P], BF16, name=f"w_sb{a}") for a in range(BLOCKS)]
         bias = held.tile([P, BLOCKS], F32, name="bias")
-        nc.sync.dma_start(bias[:], b.rearrange("(a p) o -> p (a o)", p=P))
+        for a in range(BLOCKS):
+            nc.sync.dma_start(
+                w_sb[a][:], w[:, :, a * P : (a + 1) * P].rearrange("e k m -> k e m")
+            )
+            if a == 0:
+                nc.sync.dma_start(bias[:], b.rearrange("(a p) o -> p (a o)", p=P))
 
         idle_sb = held.tile([P, S], BF16, name="idle_sb")
         nc.vector.memset(idle_sb[:], 0.0)
@@ -61,7 +65,7 @@ def tile_scatter_matmul_kernel(tc, base, x, w, b, offs, out):
             for e in range(E):
                 nc.tensor.matmul(
                     windows[a][:].indirect(offsets[:, e * QC : (e + 1) * QC]),
-                    w_sb[:, e, a * P : (a + 1) * P],
+                    w_sb[a][:, e, :],
                     x_sb[:, e * Q : (e + 1) * Q],
                     start=True,
                     stop=True,

@@ -74,5 +74,4 @@ def tile_scatter_matmul_kernel(tc, base, x, w, b, offs, out):
         for a in range(BLOCKS):
             result = held.tile([P, S], F32, name=f"result{a}")
             nc.scalar.activation(result[:], windows[a][:], TANH, bias=bias[:, a : a + 1])
-            store_queue = nc.scalar if a == BLOCKS - 1 else nc.sync
-            store_queue.dma_start(out[a * P : (a + 1) * P, :], result[:])
+            nc.sync.dma_start(out[a * P : (a + 1) * P, :], result[:])

@@ -13,8 +13,6 @@ Q = N // E
 BLOCKS = M // P
 QC = Q // 16
 
-WARM = 6
-
 FLOPS = 2 * P * M * N
 
 
@@ -42,12 +40,6 @@ def tile_scatter_matmul_kernel(tc, base, x, w, b, offs, out):
             )
             if a == 0:
                 nc.sync.dma_start(bias[:], b.rearrange("(a p) o -> p (a o)", p=P))
-
-        idle_sb = held.tile([P, S], BF16, name="idle_sb")
-        nc.vector.memset(idle_sb[:], 0.0)
-        idle_ps = banks.tile([P, S], F32, name="idle_ps")
-        for i in range(WARM):
-            nc.tensor.matmul(idle_ps[:], idle_sb[:, 0:P], idle_sb[:], start=True, stop=True)
 
         zeros = held.tile([P, 1], F32, name="zeros")
         nc.vector.memset(zeros[:], 0.0)

@@ -29,16 +29,15 @@ def tile_scatter_matmul_kernel(tc, base, x, w, b, offs, out):
         offsets = held.tile([P, N // 16], U16, name="offsets")
         nc.sync.dma_start(offsets[:], offs)
 
-        x_sb = held.tile([P, N], BF16, name="x_sb")
-        nc.sync.dma_start(x_sb[:], x)
-
         w_sb = [held.tile([P, E, P], BF16, name=f"w_sb{a}") for a in range(BLOCKS)]
+        x_sb = held.tile([P, N], BF16, name="x_sb")
         bias = held.tile([P, BLOCKS], F32, name="bias")
         for a in range(BLOCKS):
             nc.sync.dma_start(
                 w_sb[a][:], w[:, :, a * P : (a + 1) * P].rearrange("e k m -> k e m")
             )
             if a == 0:
+                nc.sync.dma_start(x_sb[:], x)
                 nc.sync.dma_start(bias[:], b.rearrange("(a p) o -> p (a o)", p=P))
 
         zeros = held.tile([P, 1], F32, name="zeros")

import concourse.mybir as mybir
from concourse.masks import make_identity

BF16, F32, U16 = mybir.dt.bfloat16, mybir.dt.float32, mybir.dt.uint16
TANH = mybir.ActivationFunctionType.Tanh

P = 128
S = 256
M = 256
N = 128
E = 2
Q = N // E
BLOCKS = M // P
QC = Q // 16

FLOPS = 2 * P * M * N


def tile_scatter_matmul_kernel(tc, base, x, w, b, offs, out):
    nc = tc.nc
    with (
        tc.tile_pool(name="held", bufs=1) as held,
        tc.psum_pool(name="banks", bufs=1) as banks,
    ):

        base_sb = held.tile([P, BLOCKS, S], BF16, name="base_sb")
        nc.sync.dma_start(base_sb[:], base.rearrange("(a p) s -> p a s", p=P))

        offsets = held.tile([P, N // 16], U16, name="offsets")
        nc.sync.dma_start(offsets[:], offs)

        w_sb = [held.tile([P, E, P], BF16, name=f"w_sb{a}") for a in range(BLOCKS)]
        x_sb = held.tile([P, N], BF16, name="x_sb")
        bias = held.tile([P, BLOCKS], F32, name="bias")
        for a in range(BLOCKS):
            nc.sync.dma_start(
                w_sb[a][:], w[:, :, a * P : (a + 1) * P].rearrange("e k m -> k e m")
            )
            if a == 0:
                nc.sync.dma_start(x_sb[:], x)
                nc.sync.dma_start(bias[:], b.rearrange("(a p) o -> p (a o)", p=P))

        zeros = held.tile([P, 1], F32, name="zeros")
        nc.vector.memset(zeros[:], 0.0)
        warmed = held.tile([P, 1], F32, name="warmed")
        nc.scalar.activation(warmed[:], zeros[:], TANH)

        ident = held.tile([P, P], BF16, name="ident")
        make_identity(nc, ident[:])

        windows = [banks.tile([P, S], F32, name=f"window{a}") for a in range(BLOCKS)]
        for a in range(BLOCKS):
            nc.tensor.matmul(windows[a][:], ident[:], base_sb[:, a, :], start=True, stop=True)

        for a in range(BLOCKS):
            for e in range(E):
                nc.tensor.matmul(
                    windows[a][:].indirect(offsets[:, e * QC : (e + 1) * QC]),
                    w_sb[a][:, e, :],
                    x_sb[:, e * Q : (e + 1) * Q],
                    start=True,
                    stop=True,
                )

        for a in range(BLOCKS):
            result = held.tile([P, S], F32, name=f"result{a}")
            nc.scalar.activation(result[:], windows[a][:], TANH, bias=bias[:, a : a + 1])
            nc.sync.dma_start(out[a * P : (a + 1) * P, :], result[:])
